import numpy as np, ml_dtypes
CORES = [16,32,48,64,80]
N = 5
import mx_ref
BF = ml_dtypes.bfloat16
def entries(a):
    return np.ascontiguousarray(a.T).reshape(-1)
def table(e):
    return np.ascontiguousarray(np.reshape(e, (-1, 16)).T).astype(np.int32)
def gpick(z, e):
    return np.concatenate([z[16 * g:16 * g + 16][:, e[g]] for g in range(8)])
def tile(rs):
    return np.stack(rs, axis=2).reshape(128, -1).astype(BF)
def cut(t, i, w=512):
    return t[:, w * i:w * i + w]
def f(rng, *shape):
    return mx_ref.flush((rng.standard_normal(shape, dtype=np.float32) * np.exp2(rng.integers(-2, 3, shape[:-1] + (1,)))).astype(BF))
def wide(rng, *shape, cols=0):
    v = rng.standard_normal(shape, dtype=np.float32) * np.exp2(rng.integers(-12, 13, shape)).astype(np.float32)
    if cols: v *= np.repeat(np.exp2(rng.integers(-cols, cols + 1, shape[:-2] + (1, shape[-1] // 4))) * (rng.random(shape[:-2] + (1, shape[-1] // 4)) > 0.0625), 4, axis=-1).astype(np.float32)
    return mx_ref.flush(v.astype(BF))
TQ, O = 384, 1
def lay(k, q):
    return {"kp": np.repeat(k, 16, axis=1).astype(np.int32), "qp": np.stack([table(e) for e in q])}
def setup_inputs(rng):
    d = {"qx": f(rng, N, 128, 4 * TQ), "ky": f(rng, N, 128, 2048), "rt": np.repeat(f(rng, 1, 128, 1024), N, axis=0), "vv": f(rng, N, 128, 512 * O)}
    a = rng.integers(0, 3585)
    k = a + rng.integers(0, 512, (N, 8, 4))
    q = np.where(rng.random((N, TQ)) < 0.25, rng.integers(0, 4096, (N, TQ)), a + rng.integers(0, 512, (N, TQ)))
    return {**d, **lay(k, q)}
def setup_inputs_far(rng):
    d = setup_inputs(rng)
    k = rng.integers(1500, 2501, (N, 32)); q = np.zeros((N, TQ), int); a = int(rng.integers(0, 2))
    for r in range(N):
        k[r, rng.permutation(32)[:2]] = [1500, 2500]
        lo, hi = (2628, 4095) if (r + a) % 2 else (0, 1371)
        q[r] = rng.integers(lo, hi + 1, TQ)
        q[r, rng.permutation(TQ)[:2]] = [lo, hi]
    return {**d, **lay(k.reshape(N, 8, 4), q)}
def setup_inputs_same(rng):
    d = setup_inputs(rng); a = int(rng.integers(0, 4096))
    return {**d, **lay(np.full((N, 8, 4), a), np.full((N, TQ), a))}
def setup_inputs_descending(rng):
    d = setup_inputs(rng); a = rng.integers(0, 3585)
    q = np.stack([a + np.sort(rng.permutation(512)[:TQ])[::-1] for r in range(N)])
    k = np.stack([a + 16 * rng.permutation(32) + rng.integers(0, 16, 32) for r in range(N)])
    return {**d, **lay(k.reshape(N, 8, 4), q)}
def setup_inputs_near(rng):
    d = setup_inputs(rng); a = rng.integers(2049, 3968)
    q = np.stack([a + rng.permutation(TQ) % 128 for r in range(N)])
    k = np.stack([a + rng.permutation(np.concatenate([[0, 128], 1 + rng.permutation(127)[:30]])) for r in range(N)])
    return {**d, **lay(k.reshape(N, 8, 4), q)}
def setup_inputs_spread(rng):
    d = setup_inputs(rng); d["qx"] = wide(rng, N, 128, 4 * TQ, cols=4); return d
def check_inputs(d):
    b = []
    for r in range(N):
        k, q = d["kp"][r], entries(d["qp"][r])
        if d["rt"][r].tobytes() != d["rt"][0].tobytes(): b.append("rt")
        if k.min() < 0 or k.max() > 4095 or (k != np.repeat(k[::16], 16, axis=0)).any(): b.append("kp")
        if q.min() < 0 or q.max() > 4095: b.append("qp")
    return b
def reference(qx, ky, rt, vv, kp, qp):
    y = np.zeros((N, 128, O * TQ), np.float32)
    X = [mx_ref.quantize(qx[r]) for r in range(N)]
    for s in range(N):
        K = [mx_ref.quantize(np.ascontiguousarray(cut(ky[s], b))) for b in range(4)]
        V = [mx_ref.quantize(np.ascontiguousarray(cut(vv[s], o))) for o in range(O)]
        R = mx_ref.quantize(rt[s])
        P = [mx_ref.matmul(K[b], R) for b in range(4)]
        for r in range(N):
            A = []
            for b in range(4):
                c = np.clip(entries(qp[r])[None, :] - kp[s][::16, b][:, None], -128, 127) + 128
                A.append(np.maximum(mx_ref.matmul(K[b], X[r]) + gpick(P[b], c), np.float32(0)) * np.float32(0.03125))
            A = mx_ref.quantize(tile(A))
            for o in range(O): y[r][:, TQ * o:TQ * o + TQ] += mx_ref.matmul(V[o], A)
    return {"y": y}

@@ -1,0 +1,292 @@
+from concourse.bass import DstId, RemoteDMATransfer
+from concourse.mybir import dt, AluOpType, ActivationFunctionType
+
+N = 5
+TQ = 384
+RT = 256
+XW = TQ + RT
+HALF = TQ // 2
+
+SCRATCH = {
+    "kyb": ("sbuf", [128, 2048], "bfloat16"),
+    "qxb": ("sbuf", [128, 4 * TQ], "bfloat16"),
+    "rtb": ("sbuf", [128, 4 * RT], "bfloat16"),
+    "vvb": ("sbuf", [128, 512], "bfloat16"),
+    "ko": ("sbuf", [128, 512], "float8_e4m3fn_x4"),
+    "kos": ("sbuf", [128, 512], "uint8"),
+    "kc": ("sbuf", [128, 512], "float8_e4m3fn_x4"),
+    "kcs": ("sbuf", [128, 512], "uint8"),
+    "xc": ("sbuf", [128, XW], "float8_e4m3fn_x4"),
+    "xs": ("sbuf", [128, XW], "uint8"),
+    "vo": ("sbuf", [128, 128], "float8_e4m3fn_x4"),
+    "vos": ("sbuf", [128, 128], "uint8"),
+    "vr": ("sbuf", [128, 512], "float8_e4m3fn_x4"),
+    "vrs": ("sbuf", [128, 512], "uint8"),
+    "ar": ("sbuf", [128, 3 * TQ], "float8_e4m3fn_x4"),
+    "ars": ("sbuf", [128, 3 * TQ], "uint8"),
+    "kpo": ("sbuf", [128, 4], "int32"),
+    "kpr": ("sbuf", [128, 4], "int32"),
+    "qr": ("sbuf", [128, 24], "int32"),
+    "ysb": ("sbuf", [128, TQ], "float32"),
+    "pb0": ("psum", [128, 512], "float32"),
+    "pb1": ("psum", [128, 512], "float32"),
+    "sb0": ("psum", [128, 512], "float32"),
+    "sb1": ("psum", [128, 512], "float32"),
+    "sb2": ("psum", [128, 512], "float32"),
+    "sb3": ("psum", [128, 512], "float32"),
+    "yb0": ("psum", [128, 512], "float32"),
+    "yb1": ("psum", [128, 512], "float32"),
+}
+for _u in range(2):
+    SCRATCH["kf%d" % _u] = ("sbuf", [128, 4], "float32")
+    SCRATCH["ot%d" % _u] = ("sbuf", [128, 96], "float32")
+    SCRATCH["om%d" % _u] = ("sbuf", [128, 96], "float32")
+    SCRATCH["off%d" % _u] = ("sbuf", [128, 96], "uint16")
+    SCRATCH["pw%d" % _u] = ("sbuf", [128, 4 * RT], "float32")
+    SCRATCH["pk%d" % _u] = ("sbuf", [128, 4 * TQ], "float32")
+    SCRATCH["at%d" % _u] = ("sbuf", [128, 4 * TQ], "bfloat16")
+    SCRATCH["ac%d" % _u] = ("sbuf", [128, TQ], "float8_e4m3fn_x4")
+    SCRATCH["as%d" % _u] = ("sbuf", [128, TQ], "uint8")
+
+SEMAPHORES = ["l_k0", "l_k1", "l_rt", "l_qx", "l_vv", "l_kp", "l_qp",
+              "q_k0", "q_k1", "q_rt", "q_qx", "q_vv",
+              "r_kp", "r_k01", "r_ks", "r_k23", "r_x", "r_q", "r_v1", "r_v2", "r_v3", "r_v4", "r_a1", "r_a2", "r_a3",
+              "sent", "m_y0", "m_y1", "c_y0", "c_y1", "st0", "st1"]
+for _u in range(2):
+    SEMAPHORES += ["%s%d" % (_n, _u) for _n in ("o_k", "o_t", "o_m", "o_o", "rl", "qa")]
+    SEMAPHORES += ["%s%d%d" % (_n, _u, _b) for _n in ("m_p", "m_s", "c_p", "ga", "ad") for _b in range(4)]
+
+
+def bits(es):
+    return sum(1 << e for e in es)
+
+
+def team(rank_core, topo):
+    mine = topo.cores_of(rank_core)
+    near = [c for c in mine if c != rank_core and topo.die(c) == topo.die(rank_core)]
+    far = [c for c in mine if topo.die(c) != topo.die(rank_core)]
+    return near[:3], far[0]
+
+
+def rank_program(g, core, T, topo):
+    v, sc, pe, sy = g.vector, g.scalar, g.tensor, g.sync
+    cores = list(T.cores)
+    teams = [team(c, topo) for c in cores]
+    role, r = None, None
+    for i, c in enumerate(cores):
+        if core == c:
+            role, r = "R", i
+        elif core in teams[i][0]:
+            role, r = "H", i
+        elif core == teams[i][1]:
+            role, r = "G", i
+    if role is None:
+        return
+    sent = [0]
+
+    def at(i):
+        return i % N
+
+    def wait(queue, name, n=1):
+        queue.wait_ge(T.sem[name], n)
+
+    def inc(ins, name, n=1):
+        ins.then_inc(T.sem[name], n)
+
+    def move(dsts, outs, src, sem, es):
+        ids = []
+        for c in dsts:
+            a = topo.addr(c)
+            ids.append(DstId(rid=a[0], pnc=a[1]))
+        sent[0] += len(es)
+        return RemoteDMATransfer(dst_ids=ids, dma_engine_mask=bits(es), remote_sem=T.sem[sem], srcs=[src], dsts=list(outs))
+
+    def send(*moves):
+        g.remote_dma_fused(list(moves), local_sem=T.sem["sent"])
+
+    def by(t):
+        return t.bitcast(dt.uint8)
+
+    def offsets(u, kp, kp_event, q_event):
+        kf, ot, om, off = T["kf%d" % u], T["ot%d" % u], T["om%d" % u], T["off%d" % u]
+        wait(v, *kp_event)
+        inc(v.tensor_copy(kf[:], kp[:]), "o_k%d" % u)
+        wait(v, *q_event)
+        wait(v, "o_k%d" % u)
+        for b in range(4):
+            inc(v.tensor_scalar(ot[:, 24 * b:24 * b + 24], T.qr[:], kf[:, b:b + 1], -128.0, AluOpType.subtract, AluOpType.max), "o_t%d" % u)
+        wait(v, "o_t%d" % u, 4)
+        inc(v.tensor_scalar(om[:], ot[:], 127.0, 128.0, AluOpType.min, AluOpType.add), "o_m%d" % u)
+        wait(v, "o_m%d" % u)
+        inc(v.tensor_copy(off[:], om[:]), "o_o%d" % u)
+
+    def products(u, kc, ks, events_p, events_s):
+        for h in range(2):
+            for e in events_p[h]:
+                wait(pe, *e)
+            for b in (2 * h, 2 * h + 1):
+                if b >= 2:
+                    wait(pe, "c_p%d%d" % (u, b - 2))
+                elif u:
+                    wait(pe, "c_p%d%d" % (u - 1, b + 2))
+                inc(pe.matmul_mx(T["pb%d" % (b % 2)][:, 0:RT], kc[:, 128 * b:128 * b + 128], ks[:, 128 * b:128 * b + 128],
+                                 T.xc[:, TQ:XW], T.xs[:, TQ:XW], True, True), "m_p%d%d" % (u, b))
+            for e in events_s[h]:
+                wait(pe, *e)
+            for b in (2 * h, 2 * h + 1):
+                if u:
+                    wait(pe, "ad%d%d" % (u - 1, b))
+                inc(pe.matmul_mx(T["sb%d" % b][:, 0:TQ], kc[:, 128 * b:128 * b + 128], ks[:, 128 * b:128 * b + 128],
+                                 T.xc[:, 0:TQ], T.xs[:, 0:TQ], True, True), "m_s%d%d" % (u, b))
+
+    def picks(u):
+        pw, pk, off = T["pw%d" % u], T["pk%d" % u], T["off%d" % u]
+        wait(sc, "o_o%d" % u)
+        for b in range(4):
+            wait(sc, "c_p%d%d" % (u, b))
+            inc(sc.activation(pk[:, TQ * b:TQ * b + TQ], pw[:, RT * b:RT * b + RT].indirect(off[:, 24 * b:24 * b + 24]),
+                              ActivationFunctionType.Copy), "ga%d%d" % (u, b))
+
+    def copy_p(u, b):
+        wait(v, "m_p%d%d" % (u, b))
+        inc(v.tensor_copy(T["pw%d" % u][:, RT * b:RT * b + RT], T["pb%d" % (b % 2)][:, 0:RT]), "c_p%d%d" % (u, b))
+
+    def add_relu(u, b):
+        col = T["at%d" % u][:, b:4 * TQ:4]
+        wait(v, "m_s%d%d" % (u, b))
+        wait(v, "ga%d%d" % (u, b))
+        inc(v.tensor_tensor(col, T["sb%d" % b][:, 0:TQ], T["pk%d" % u][:, TQ * b:TQ * b + TQ], AluOpType.add), "ad%d%d" % (u, b))
+        wait(v, "ad%d%d" % (u, b))
+        inc(v.tensor_scalar(col, col, 0.0, 0.03125, AluOpType.max, AluOpType.mult), "rl%d" % u)
+
+    def pack(u):
+        wait(v, "rl%d" % u, 4)
+        inc(v.quantize_mx(T["ac%d" % u][:], T["as%d" % u][:], T["at%d" % u][:]), "qa%d" % u)
+
+    def elementwise(u, order):
+        for step, b in order:
+            (copy_p if step == "c" else add_relu)(u, b)
+        pack(u)
+
+    HALVES = [("c", 0), ("c", 1), ("a", 0), ("a", 1), ("c", 2), ("c", 3), ("a", 2), ("a", 3)]
+    ALL = [("c", 0), ("c", 1), ("c", 2), ("c", 3), ("a", 0), ("a", 1), ("a", 2), ("a", 3)]
+
+    near, far = teams[r]
+    if role == "G":
+        d3, d4 = teams[at(r + 3)][0][2], cores[at(r + 4)]
+        es = topo.engines(core, d3)
+        nk = len([e for e in topo.engines(cores[r], core) if e not in topo.engines(cores[r], d3)])
+        wait(g, "r_k01", nk)
+        send(move([d3, d4], [by(T.kc[:, 0:256])] * 2, by(T.kc[:, 0:256]), "r_k01", es))
+        wait(g, "r_ks", nk)
+        send(move([d3, d4], [T.kcs[:]] * 2, T.kcs[:], "r_ks", es))
+        wait(g, "r_k23", nk)
+        send(move([d3, d4], [by(T.kc[:, 256:512])] * 2, by(T.kc[:, 256:512]), "r_k23", es))
+        wait(g, "sent", sent[0])
+        return
+
+    out = topo.engines(cores[r], cores[at(r + 1)])
+    stay = [e for e in topo.engines(cores[r], far) if e not in out]
+    first = [("r_k01", len(out)), ("r_ks", len(out))]
+    second = [("r_k23", len(out))]
+
+    if role == "H":
+        d = near.index(core) + 1
+        nx = 2 * (len(stay) if d < 3 else len(out))
+        offsets(0, T.kpr, ("r_kp", len(out)), ("r_q", len(stay)))
+        products(0, T.kc, T.kcs, [first + [("r_x", nx)], second], [[], []])
+        picks(0)
+        elementwise(0, HALVES)
+        es = topo.engines(core, cores[r])
+        wait(g, "qa0")
+        send(move([cores[r]], [by(T.ar[:, TQ * (d - 1):TQ * d])], by(T.ac0[:]), "r_a%d" % d, es))
+        send(move([cores[r]], [T.ars[:, TQ * (d - 1):TQ * d]], T.as0[:], "r_a%d" % d, es))
+        wait(g, "sent", sent[0])
+        return
+
+    inc(sy.dma_start(T.kpo[:], T.kp[:]), "l_kp", 16)
+    inc(sy.dma_start(T.kyb[:, 0:1024], T.ky[:, 0:1024]), "l_k0", 16)
+    inc(sy.dma_start(T.kyb[:, 1024:2048], T.ky[:, 1024:2048]), "l_k1", 16)
+    inc(sy.dma_start(T.rtb[:], T.rt[:]), "l_rt", 16)
+    inc(sy.dma_start(T.qxb[:], T.qx[:]), "l_qx", 16)
+    inc(sy.dma_start(T.vvb[:], T.vv[:]), "l_vv", 16)
+    for q in range(8):
+        inc(sc.dma_start(T.qr[16 * q:16 * q + 16, :], T.qp[:]), "l_qp", 16)
+
+    d1, d2, d3 = [teams[at(r + d)][0][d - 1] for d in (1, 2, 3)]
+    d4 = cores[at(r + 4)]
+    wait(g, "l_kp", 16)
+    send(move([d1, d2, d3, d4], [T.kpr[:]] * 4, T.kpo[:], "r_kp", out))
+
+    def keys(dst, src, sem):
+        send(move([d1, d2], [dst] * 2, src, sem, out), move([far], [dst], src, sem, stay))
+
+    wait(g, "q_k0")
+    keys(by(T.kc[:, 0:256]), by(T.ko[:, 0:256]), "r_k01")
+    wait(g, "q_k1")
+    keys(T.kcs[:], T.kos[:], "r_ks")
+    keys(by(T.kc[:, 256:512]), by(T.ko[:, 256:512]), "r_k23")
+    wait(g, "l_qp", 128)
+    send(move(near, [T.qr[:]] * 3, T.qr[:], "r_q", stay))
+    wait(g, "q_rt")
+    wait(g, "q_qx")
+    for a in (by(T.xc[:]), T.xs[:]):
+        send(move(near[:2], [a] * 2, a, "r_x", stay), move(near[2:], [a], a, "r_x", out))
+    wait(g, "q_vv")
+    per = len(out) // 4
+    for own, there, f in ((T.vo, T.vr, by), (T.vos, T.vrs, lambda t: t)):
+        send(*[move([cores[at(r + d)]], [f(there[:, 128 * (d - 1):128 * d])], f(own[:]), "r_v%d" % d, out[per * (d - 1):per * d])
+               for d in (1, 2, 3, 4)])
+    wait(g, "sent", sent[0])
+
+    for name, codes, plane, tile in (("k0", T.ko[:, 0:256], T.kos[:, 0:256], T.kyb[:, 0:1024]),
+                                     ("k1", T.ko[:, 256:512], T.kos[:, 256:512], T.kyb[:, 1024:2048]),
+                                     ("rt", T.xc[:, TQ:XW], T.xs[:, TQ:XW], T.rtb[:]),
+                                     ("qx", T.xc[:, 0:TQ], T.xs[:, 0:TQ], T.qxb[:])):
+        wait(v, "l_" + name, 16)
+        inc(v.quantize_mx(codes, plane, tile), "q_" + name)
+    offsets(0, T.kpo, ("l_kp", 16), ("l_qp", 128))
+    elementwise(0, ALL)
+    wait(v, "l_vv", 16)
+    inc(v.quantize_mx(T.vo[:], T.vos[:], T.vvb[:]), "q_vv")
+    offsets(1, T.kpr, ("r_kp", len(out)), ("l_qp", 128))
+    elementwise(1, HALVES)
+
+    picks(0)
+    picks(1)
+
+    def value(vc, vs, ac, as_, a, start, stop):
+        for h in range(2):
+            ins = pe.matmul_mx(T["yb%d" % h][:, 0:HALF], vc, vs, ac[:, a + HALF * h:a + HALF * h + HALF],
+                               as_[:, a + HALF * h:a + HALF * h + HALF], start, stop)
+            if stop:
+                inc(ins, "m_y%d" % h)
+
+    def slot(d):
+        return T.vr[:, 128 * (d - 1):128 * d], T.vrs[:, 128 * (d - 1):128 * d]
+
+    products(0, T.ko, T.kos, [[("q_k0", 1), ("q_rt", 1)], [("q_k1", 1)]], [[("q_qx", 1)], []])
+    wait(pe, "qa0")
+    wait(pe, "q_vv")
+    value(T.vo[:], T.vos[:], T.ac0, T.as0, 0, True, False)
+    products(1, T.kc, T.kcs, [first, second], [[], []])
+    na = 2 * len(topo.engines(near[0], core))
+    for d in (1, 2, 4, 3):
+        wait(pe, "r_v%d" % d, 2 * per)
+        if d == 4:
+            wait(pe, "qa1")
+            value(*slot(d), T.ac1, T.as1, 0, False, False)
+        else:
+            wait(pe, "r_a%d" % d, na)
+            value(*slot(d), T.ar, T.ars, TQ * (d - 1), False, d == 3)
+
+    wait(v, "m_y0")
+    inc(v.tensor_copy(T.ysb[:, 0:HALF], T.yb0[:, 0:HALF]), "c_y0")
+    wait(sc, "m_y1")
+    inc(sc.activation(T.ysb[:, HALF:TQ], T.yb1[:, 0:HALF], ActivationFunctionType.Copy), "c_y1")
+    wait(sy, "c_y0")
+    inc(sy.dma_start(T.y[:, 0:HALF], T.ysb[:, 0:HALF]), "st0", 16)
+    wait(sc, "c_y1")
+    inc(sc.dma_start(T.y[:, HALF:TQ], T.ysb[:, HALF:TQ]), "st1", 16)
+    wait(sy, "st0", 16)
+    wait(sc, "st1", 16)

@@ -14,6 +14,7 @@ SCRATCH = {
     "vvb": ("sbuf", [128, 512], "bfloat16"),
     "ko": ("sbuf", [128, 512], "float8_e4m3fn_x4"),
     "kos": ("sbuf", [128, 512], "uint8"),
+    "kw": ("sbuf", [128, 128], "float8_e4m3fn_x4"),
     "kc": ("sbuf", [128, 512], "float8_e4m3fn_x4"),
     "kcs": ("sbuf", [128, 512], "uint8"),
     "xc": ("sbuf", [128, XW], "float8_e4m3fn_x4"),
@@ -25,18 +26,14 @@ SCRATCH = {
     "ar": ("sbuf", [128, 3 * TQ], "float8_e4m3fn_x4"),
     "ars": ("sbuf", [128, 3 * TQ], "uint8"),
     "kpo": ("sbuf", [128, 4], "int32"),
+    "kpf": ("sbuf", [128, 4], "int32"),
     "kpr": ("sbuf", [128, 4], "int32"),
     "qr": ("sbuf", [128, 24], "int32"),
     "ysb": ("sbuf", [128, TQ], "float32"),
-    "pb0": ("psum", [128, 512], "float32"),
-    "pb1": ("psum", [128, 512], "float32"),
-    "sb0": ("psum", [128, 512], "float32"),
-    "sb1": ("psum", [128, 512], "float32"),
-    "sb2": ("psum", [128, 512], "float32"),
-    "sb3": ("psum", [128, 512], "float32"),
-    "yb0": ("psum", [128, 512], "float32"),
-    "yb1": ("psum", [128, 512], "float32"),
 }
+BANKS = ["pb0", "pb1", "yb0", "yb1", "sb0", "sb1", "sb2", "sb3"]
+for _n in BANKS:
+    SCRATCH[_n] = ("psum", [128, 512], "float32")
 for _u in range(2):
     SCRATCH["kf%d" % _u] = ("sbuf", [128, 4], "float32")
     SCRATCH["ot%d" % _u] = ("sbuf", [128, 96], "float32")
@@ -50,11 +47,14 @@ for _u in range(2):
 
 SEMAPHORES = ["l_k0", "l_k1", "l_rt", "l_qx", "l_vv", "l_kp", "l_qp",
               "q_k0", "q_k1", "q_rt", "q_qx", "q_vv",
-              "r_kp", "r_k01", "r_ks", "r_k23", "r_x", "r_q", "r_v1", "r_v2", "r_v3", "r_v4", "r_a1", "r_a2", "r_a3",
+              "r_kpf", "r_kp", "r_kw", "r_k0", "r_k1", "r_k2", "r_k3", "r_ks", "r_x", "r_q",
+              "r_vc", "r_vs", "r_v1", "r_v2", "r_v3", "r_v4", "r_a10", "r_a11", "r_a20", "r_a21", "r_a30", "r_a31",
               "sent", "m_y0", "m_y1", "c_y0", "c_y1", "st0", "st1"]
 for _u in range(2):
-    SEMAPHORES += ["%s%d" % (_n, _u) for _n in ("o_k", "o_t", "o_m", "o_o", "rl", "qa")]
-    SEMAPHORES += ["%s%d%d" % (_n, _u, _b) for _n in ("m_p", "m_s", "c_p", "ga", "ad") for _b in range(4)]
+    SEMAPHORES += ["%s%d" % (_n, _u) for _n in ("o_k", "o_t", "o_m", "o_o", "rb")]
+    SEMAPHORES += ["%s%d%d" % (_n, _u, _h) for _n in ("rl", "qa") for _h in range(2)]
+    SEMAPHORES += ["%s%d%d" % (_n, _u, _b) for _n in ("m_p", "m_s", "c_p") for _b in range(4)]
+    SEMAPHORES += ["%s%d%d%d" % (_n, _u, _b, _h) for _n in ("ga", "ad") for _b in range(4) for _h in range(2)]
 
 
 def bits(es):
@@ -65,27 +65,34 @@ def team(rank_core, topo):
     mine = topo.cores_of(rank_core)
     near = [c for c in mine if c != rank_core and topo.die(c) == topo.die(rank_core)]
     far = [c for c in mine if topo.die(c) != topo.die(rank_core)]
-    return near[:3], far[0]
+    return near[:3], far
 
 
 def rank_program(g, core, T, topo):
     v, sc, pe, sy = g.vector, g.scalar, g.tensor, g.sync
     cores = list(T.cores)
     teams = [team(c, topo) for c in cores]
-    role, r = None, None
+    r = None
     for i, c in enumerate(cores):
-        if core == c:
-            role, r = "R", i
-        elif core in teams[i][0]:
-            role, r = "H", i
-        elif core == teams[i][1]:
-            role, r = "G", i
-    if role is None:
+        if core == c or core in teams[i][0] or core in teams[i][1]:
+            r = i
+    if r is None:
         return
+    me = cores[r]
+    near, far = teams[r]
+    relays = [far[0], near[0], far[1], near[1]]
+    posts = [far[0], near[0], near[2], near[1]]
+    out = topo.engines(me, cores[(r + 1) % N])
+    every = topo.engines(me, far[0])
+    stay = [e for e in every if e not in out]
+    few = len(stay) // 2
     sent = [0]
 
-    def at(i):
-        return i % N
+    def worker(s, d):
+        i = (s + d) % N
+        return teams[i][0][d - 1] if d < 4 else cores[i]
+
+    users = [worker(r, d) for d in (1, 2, 3, 4)]
 
     def wait(queue, name, n=1):
         queue.wait_ge(T.sem[name], n)
@@ -120,87 +127,114 @@ def rank_program(g, core, T, topo):
         wait(v, "o_m%d" % u)
         inc(v.tensor_copy(off[:], om[:]), "o_o%d" % u)
 
-    def products(u, kc, ks, events_p, events_s):
+    def products(u, kc, ks, banks, events, events_x):
         for h in range(2):
-            for e in events_p[h]:
-                wait(pe, *e)
             for b in (2 * h, 2 * h + 1):
-                if b >= 2:
-                    wait(pe, "c_p%d%d" % (u, b - 2))
+                for e in events[b]:
+                    wait(pe, *e)
+                if b >= banks:
+                    wait(pe, "c_p%d%d" % (u, b - banks))
                 elif u:
+                    wait(pe, "c_p%d%d" % (u - 1, b))
                     wait(pe, "c_p%d%d" % (u - 1, b + 2))
-                inc(pe.matmul_mx(T["pb%d" % (b % 2)][:, 0:RT], kc[:, 128 * b:128 * b + 128], ks[:, 128 * b:128 * b + 128],
+                inc(pe.matmul_mx(T[BANKS[b % banks]][:, 0:RT], kc[:, 128 * b:128 * b + 128], ks[:, 128 * b:128 * b + 128],
                                  T.xc[:, TQ:XW], T.xs[:, TQ:XW], True, True), "m_p%d%d" % (u, b))
-            for e in events_s[h]:
+            for e in events_x:
                 wait(pe, *e)
             for b in (2 * h, 2 * h + 1):
                 if u:
-                    wait(pe, "ad%d%d" % (u - 1, b))
+                    wait(pe, "ad%d%d0" % (u - 1, b))
+                    wait(pe, "ad%d%d1" % (u - 1, b))
                 inc(pe.matmul_mx(T["sb%d" % b][:, 0:TQ], kc[:, 128 * b:128 * b + 128], ks[:, 128 * b:128 * b + 128],
                                  T.xc[:, 0:TQ], T.xs[:, 0:TQ], True, True), "m_s%d%d" % (u, b))
 
-    def picks(u):
-        pw, pk, off = T["pw%d" % u], T["pk%d" % u], T["off%d" % u]
+    def copy_p(queue, u, b, banks):
+        bank, window = T[BANKS[b % banks]][:, 0:RT], T["pw%d" % u][:, RT * b:RT * b + RT]
+        wait(queue, "m_p%d%d" % (u, b))
+        if queue is v:
+            ins = v.tensor_copy(window, bank)
+        else:
+            ins = sc.activation(window, bank, ActivationFunctionType.Copy)
+        inc(ins, "c_p%d%d" % (u, b))
+
+    def pick(u, b, h):
+        off, at = T["off%d" % u], 24 * b + 12 * h
+        wait(sc, "c_p%d%d" % (u, b))
+        inc(sc.activation(T["pk%d" % u][:, TQ * b + HALF * h:TQ * b + HALF * h + HALF],
+                          T["pw%d" % u][:, RT * b:RT * b + RT].indirect(off[:, at:at + 12]), ActivationFunctionType.Copy), "ga%d%d%d" % (u, b, h))
+
+    def picks(u, banks):
+        copy_p(sc, u, 0, banks)
         wait(sc, "o_o%d" % u)
-        for b in range(4):
-            wait(sc, "c_p%d%d" % (u, b))
-            inc(sc.activation(pk[:, TQ * b:TQ * b + TQ], pw[:, RT * b:RT * b + RT].indirect(off[:, 24 * b:24 * b + 24]),
-                              ActivationFunctionType.Copy), "ga%d%d" % (u, b))
+        for b, h in ((0, 0), (1, 0), (0, 1), (1, 1)):
+            pick(u, b, h)
+        copy_p(sc, u, 3, banks)
+        for b, h in ((2, 0), (3, 0), (2, 1), (3, 1)):
+            pick(u, b, h)
 
-    def copy_p(u, b):
-        wait(v, "m_p%d%d" % (u, b))
-        inc(v.tensor_copy(T["pw%d" % u][:, RT * b:RT * b + RT], T["pb%d" % (b % 2)][:, 0:RT]), "c_p%d%d" % (u, b))
-
-    def add_relu(u, b):
-        col = T["at%d" % u][:, b:4 * TQ:4]
+    def add(u, b, h):
         wait(v, "m_s%d%d" % (u, b))
-        wait(v, "ga%d%d" % (u, b))
-        inc(v.tensor_tensor(col, T["sb%d" % b][:, 0:TQ], T["pk%d" % u][:, TQ * b:TQ * b + TQ], AluOpType.add), "ad%d%d" % (u, b))
-        wait(v, "ad%d%d" % (u, b))
-        inc(v.tensor_scalar(col, col, 0.0, 0.03125, AluOpType.max, AluOpType.mult), "rl%d" % u)
+        wait(v, "ga%d%d%d" % (u, b, h))
+        inc(v.tensor_tensor(T["at%d" % u][:, 4 * HALF * h + b:4 * HALF * (h + 1):4], T["sb%d" % b][:, HALF * h:HALF * h + HALF],
+                            T["pk%d" % u][:, TQ * b + HALF * h:TQ * b + HALF * h + HALF], AluOpType.add), "ad%d%d%d" % (u, b, h))
 
-    def pack(u):
-        wait(v, "rl%d" % u, 4)
-        inc(v.quantize_mx(T["ac%d" % u][:], T["as%d" % u][:], T["at%d" % u][:]), "qa%d" % u)
+    def relu(u, b, hs, sem):
+        col = T["at%d" % u][:, 4 * HALF * hs[0] + b:4 * HALF * (hs[-1] + 1):4]
+        for h in hs:
+            wait(v, "ad%d%d%d" % (u, b, h))
+        inc(v.tensor_scalar(col, col, 0.0, 0.03125, AluOpType.max, AluOpType.mult), sem)
 
-    def elementwise(u, order):
-        for step, b in order:
-            (copy_p if step == "c" else add_relu)(u, b)
-        pack(u)
+    def elementwise(u, banks):
+        copy_p(v, u, 1, banks)
+        add(u, 0, 0)
+        add(u, 1, 0)
+        copy_p(v, u, 2, banks)
+        add(u, 0, 1)
+        add(u, 1, 1)
+        relu(u, 0, (0, 1), "rb%d" % u)
+        relu(u, 1, (0, 1), "rb%d" % u)
+        for h in range(2):
+            for b in (2, 3):
+                add(u, b, h)
+                relu(u, b, (h,), "rl%d%d" % (u, h))
+            if h == 0:
+                wait(v, "rb%d" % u, 2)
+            wait(v, "rl%d%d" % (u, h), 2)
+            a, e = HALF * h, HALF * h + HALF
+            inc(v.quantize_mx(T["ac%d" % u][:, a:e], T["as%d" % u][:, a:e], T["at%d" % u][:, 4 * a:4 * e]), "qa%d%d" % (u, h))
 
-    HALVES = [("c", 0), ("c", 1), ("a", 0), ("a", 1), ("c", 2), ("c", 3), ("a", 2), ("a", 3)]
-    ALL = [("c", 0), ("c", 1), ("c", 2), ("c", 3), ("a", 0), ("a", 1), ("a", 2), ("a", 3)]
-
-    near, far = teams[r]
-    if role == "G":
-        d3, d4 = teams[at(r + 3)][0][2], cores[at(r + 4)]
-        es = topo.engines(core, d3)
-        nk = len([e for e in topo.engines(cores[r], core) if e not in topo.engines(cores[r], d3)])
-        wait(g, "r_k01", nk)
-        send(move([d3, d4], [by(T.kc[:, 0:256])] * 2, by(T.kc[:, 0:256]), "r_k01", es))
-        wait(g, "r_ks", nk)
-        send(move([d3, d4], [T.kcs[:]] * 2, T.kcs[:], "r_ks", es))
-        wait(g, "r_k23", nk)
-        send(move([d3, d4], [by(T.kc[:, 256:512])] * 2, by(T.kc[:, 256:512]), "r_k23", es))
+    if core in posts:
+        c = users[posts.index(core)]
+        wait(g, "r_kpf", len(every))
+        send(move([c], [T.kpr[:]], T.kpf[:], "r_kp", out))
+    if core in relays:
+        b = relays.index(core)
+        wait(g, "r_kw", len(stay) if b < 2 else few)
+        send(move(users, [by(T.kc[:, 128 * b:128 * b + 128])] * 4, by(T.kw[:]), "r_k%d" % b, out))
+    per = len(out) // 4
+    for c, name, own, there, f in ((far[2], "r_vc", T.vo, T.vr, by), (far[3], "r_vs", T.vos, T.vrs, lambda t: t)):
+        if core == c:
+            wait(g, name, len(stay))
+            send(*[move([cores[(r + d) % N]], [f(there[:, 128 * (d - 1):128 * d])], f(own[:]), "r_v%d" % d, out[per * (d - 1):per * d])
+                   for d in (1, 2, 3, 4)])
+    if core in far:
         wait(g, "sent", sent[0])
         return
 
-    out = topo.engines(cores[r], cores[at(r + 1)])
-    stay = [e for e in topo.engines(cores[r], far) if e not in out]
-    first = [("r_k01", len(out)), ("r_ks", len(out))]
-    second = [("r_k23", len(out))]
+    keys = [[("r_ks", len(out)), ("r_k%d" % b, len(out))] for b in range(4)]
 
-    if role == "H":
+    if core in near:
         d = near.index(core) + 1
-        nx = 2 * (len(stay) if d < 3 else len(out))
         offsets(0, T.kpr, ("r_kp", len(out)), ("r_q", len(stay)))
-        products(0, T.kc, T.kcs, [first + [("r_x", nx)], second], [[], []])
-        picks(0)
-        elementwise(0, HALVES)
-        es = topo.engines(core, cores[r])
-        wait(g, "qa0")
-        send(move([cores[r]], [by(T.ar[:, TQ * (d - 1):TQ * d])], by(T.ac0[:]), "r_a%d" % d, es))
-        send(move([cores[r]], [T.ars[:, TQ * (d - 1):TQ * d]], T.as0[:], "r_a%d" % d, es))
+        products(0, T.kc, T.kcs, 4, [keys[0] + [("r_x", 2 * len(every))]] + keys[1:], [])
+        picks(0, 4)
+        elementwise(0, 4)
+        a = TQ * (d - 1)
+        for h in range(2):
+            wait(g, "qa0%d" % h)
+            i, e = HALF * h, HALF * h + HALF
+            send(move([me], [by(T.ar[:, a + i:a + e])], by(T.ac0[:, i:e]), "r_a%d%d" % (d, h), every))
+            send(move([me], [T.ars[:, a + i:a + e]], T.as0[:, i:e], "r_a%d%d" % (d, h), every))
         wait(g, "sent", sent[0])
         return
 
@@ -208,35 +242,30 @@ def rank_program(g, core, T, topo):
     inc(sy.dma_start(T.kyb[:, 0:1024], T.ky[:, 0:1024]), "l_k0", 16)
     inc(sy.dma_start(T.kyb[:, 1024:2048], T.ky[:, 1024:2048]), "l_k1", 16)
     inc(sy.dma_start(T.rtb[:], T.rt[:]), "l_rt", 16)
-    inc(sy.dma_start(T.qxb[:], T.qx[:]), "l_qx", 16)
-    inc(sy.dma_start(T.vvb[:], T.vv[:]), "l_vv", 16)
     for q in range(8):
         inc(sc.dma_start(T.qr[16 * q:16 * q + 16, :], T.qp[:]), "l_qp", 16)
+    inc(sc.dma_start(T.qxb[:], T.qx[:]), "l_qx", 16)
+    inc(sc.dma_start(T.vvb[:], T.vv[:]), "l_vv", 16)
 
-    d1, d2, d3 = [teams[at(r + d)][0][d - 1] for d in (1, 2, 3)]
-    d4 = cores[at(r + 4)]
     wait(g, "l_kp", 16)
-    send(move([d1, d2, d3, d4], [T.kpr[:]] * 4, T.kpo[:], "r_kp", out))
+    send(move(posts, [T.kpf[:]] * 4, T.kpo[:], "r_kpf", every))
 
-    def keys(dst, src, sem):
-        send(move([d1, d2], [dst] * 2, src, sem, out), move([far], [dst], src, sem, stay))
+    def piece(b, es):
+        return move([relays[b]], [by(T.kw[:])], by(T.ko[:, 128 * b:128 * b + 128]), "r_kw", es)
 
     wait(g, "q_k0")
-    keys(by(T.kc[:, 0:256]), by(T.ko[:, 0:256]), "r_k01")
+    send(piece(0, out), piece(1, stay))
     wait(g, "q_k1")
-    keys(T.kcs[:], T.kos[:], "r_ks")
-    keys(by(T.kc[:, 256:512]), by(T.ko[:, 256:512]), "r_k23")
+    send(piece(2, stay[:few]), piece(3, stay[few:]), move(users, [T.kcs[:]] * 4, T.kos[:], "r_ks", out))
     wait(g, "l_qp", 128)
     send(move(near, [T.qr[:]] * 3, T.qr[:], "r_q", stay))
     wait(g, "q_rt")
     wait(g, "q_qx")
     for a in (by(T.xc[:]), T.xs[:]):
-        send(move(near[:2], [a] * 2, a, "r_x", stay), move(near[2:], [a], a, "r_x", out))
+        send(move(near[::-1], [a] * 3, a, "r_x", every))
     wait(g, "q_vv")
-    per = len(out) // 4
-    for own, there, f in ((T.vo, T.vr, by), (T.vos, T.vrs, lambda t: t)):
-        send(*[move([cores[at(r + d)]], [f(there[:, 128 * (d - 1):128 * d])], f(own[:]), "r_v%d" % d, out[per * (d - 1):per * d])
-               for d in (1, 2, 3, 4)])
+    send(move([far[2]], [by(T.vo[:])], by(T.vo[:]), "r_vc", stay))
+    send(move([far[3]], [T.vos[:]], T.vos[:], "r_vs", out))
     wait(g, "sent", sent[0])
 
     for name, codes, plane, tile in (("k0", T.ko[:, 0:256], T.kos[:, 0:256], T.kyb[:, 0:1024]),
@@ -246,47 +275,47 @@ def rank_program(g, core, T, topo):
         wait(v, "l_" + name, 16)
         inc(v.quantize_mx(codes, plane, tile), "q_" + name)
     offsets(0, T.kpo, ("l_kp", 16), ("l_qp", 128))
-    elementwise(0, ALL)
     wait(v, "l_vv", 16)
     inc(v.quantize_mx(T.vo[:], T.vos[:], T.vvb[:]), "q_vv")
+    elementwise(0, 4)
     offsets(1, T.kpr, ("r_kp", len(out)), ("l_qp", 128))
-    elementwise(1, HALVES)
+    elementwise(1, 2)
 
-    picks(0)
-    picks(1)
+    picks(0, 4)
+    picks(1, 2)
 
-    def value(vc, vs, ac, as_, a, start, stop):
-        for h in range(2):
-            ins = pe.matmul_mx(T["yb%d" % h][:, 0:HALF], vc, vs, ac[:, a + HALF * h:a + HALF * h + HALF],
-                               as_[:, a + HALF * h:a + HALF * h + HALF], start, stop)
-            if stop:
-                inc(ins, "m_y%d" % h)
+    def value(vc, vs, ac, as_, a, h, start, stop):
+        i, e = a + HALF * h, a + HALF * h + HALF
+        ins = pe.matmul_mx(T["yb%d" % h][:, 0:HALF], vc, vs, ac[:, i:e], as_[:, i:e], start, stop)
+        if stop:
+            inc(ins, "m_y%d" % h)
 
     def slot(d):
         return T.vr[:, 128 * (d - 1):128 * d], T.vrs[:, 128 * (d - 1):128 * d]
 
-    products(0, T.ko, T.kos, [[("q_k0", 1), ("q_rt", 1)], [("q_k1", 1)]], [[("q_qx", 1)], []])
-    wait(pe, "qa0")
-    wait(pe, "q_vv")
-    value(T.vo[:], T.vos[:], T.ac0, T.as0, 0, True, False)
-    products(1, T.kc, T.kcs, [first, second], [[], []])
-    na = 2 * len(topo.engines(near[0], core))
-    for d in (1, 2, 4, 3):
-        wait(pe, "r_v%d" % d, 2 * per)
-        if d == 4:
-            wait(pe, "qa1")
-            value(*slot(d), T.ac1, T.as1, 0, False, False)
-        else:
-            wait(pe, "r_a%d" % d, na)
-            value(*slot(d), T.ar, T.ars, TQ * (d - 1), False, d == 3)
+    products(0, T.ko, T.kos, 4, [[("q_k0", 1), ("q_rt", 1)], [], [("q_k1", 1)], []], [("q_qx", 1)])
+    for e in ("qa00", "qa01", "q_vv", "c_p02", "c_p03"):
+        wait(pe, e)
+    for h in range(2):
+        value(T.vo[:], T.vos[:], T.ac0, T.as0, 0, h, True, False)
+    products(1, T.kc, T.kcs, 2, keys, [])
+    for h in range(2):
+        for d in (4, 3, 1, 2):
+            wait(pe, "r_v%d" % d, 2 * per)
+            if d == 4:
+                wait(pe, "qa1%d" % h)
+                value(*slot(d), T.ac1, T.as1, 0, h, False, False)
+            else:
+                wait(pe, "r_a%d%d" % (d, h), 2 * len(every))
+                value(*slot(d), T.ar, T.ars, TQ * (d - 1), h, False, d == 2)
 
-    wait(v, "m_y0")
-    inc(v.tensor_copy(T.ysb[:, 0:HALF], T.yb0[:, 0:HALF]), "c_y0")
-    wait(sc, "m_y1")
-    inc(sc.activation(T.ysb[:, HALF:TQ], T.yb1[:, 0:HALF], ActivationFunctionType.Copy), "c_y1")
-    wait(sy, "c_y0")
-    inc(sy.dma_start(T.y[:, 0:HALF], T.ysb[:, 0:HALF]), "st0", 16)
-    wait(sc, "c_y1")
-    inc(sc.dma_start(T.y[:, HALF:TQ], T.ysb[:, HALF:TQ]), "st1", 16)
-    wait(sy, "st0", 16)
-    wait(sc, "st1", 16)
+    wait(sc, "m_y0")
+    inc(sc.activation(T.ysb[:, 0:HALF], T.yb0[:, 0:HALF], ActivationFunctionType.Copy), "c_y0")
+    wait(sc, "c_y0")
+    inc(sc.dma_start(T.y[:, 0:HALF], T.ysb[:, 0:HALF]), "st0", 16)
+    wait(v, "m_y1")
+    inc(v.tensor_copy(T.ysb[:, HALF:TQ], T.yb1[:, 0:HALF]), "c_y1")
+    wait(sy, "c_y1")
+    inc(sy.dma_start(T.y[:, HALF:TQ], T.ysb[:, HALF:TQ]), "st1", 16)
+    wait(sc, "st0", 16)
+    wait(sy, "st1", 16)

from concourse.bass import DstId, RemoteDMATransfer
from concourse.mybir import dt, AluOpType, ActivationFunctionType

N = 5
TQ = 384
RT = 256
XW = TQ + RT
HALF = TQ // 2

SCRATCH = {
    "kyb": ("sbuf", [128, 2048], "bfloat16"),
    "qxb": ("sbuf", [128, 4 * TQ], "bfloat16"),
    "rtb": ("sbuf", [128, 4 * RT], "bfloat16"),
    "vvb": ("sbuf", [128, 512], "bfloat16"),
    "ko": ("sbuf", [128, 512], "float8_e4m3fn_x4"),
    "kos": ("sbuf", [128, 512], "uint8"),
    "kw": ("sbuf", [128, 128], "float8_e4m3fn_x4"),
    "kc": ("sbuf", [128, 512], "float8_e4m3fn_x4"),
    "kcs": ("sbuf", [128, 512], "uint8"),
    "xc": ("sbuf", [128, XW], "float8_e4m3fn_x4"),
    "xs": ("sbuf", [128, XW], "uint8"),
    "vo": ("sbuf", [128, 128], "float8_e4m3fn_x4"),
    "vos": ("sbuf", [128, 128], "uint8"),
    "vr": ("sbuf", [128, 512], "float8_e4m3fn_x4"),
    "vrs": ("sbuf", [128, 512], "uint8"),
    "ar": ("sbuf", [128, 3 * TQ], "float8_e4m3fn_x4"),
    "ars": ("sbuf", [128, 3 * TQ], "uint8"),
    "kpo": ("sbuf", [128, 4], "int32"),
    "kpf": ("sbuf", [128, 4], "int32"),
    "kpr": ("sbuf", [128, 4], "int32"),
    "qr": ("sbuf", [128, 24], "int32"),
    "ysb": ("sbuf", [128, TQ], "float32"),
}
BANKS = ["pb0", "pb1", "yb0", "yb1", "sb0", "sb1", "sb2", "sb3"]
for _n in BANKS:
    SCRATCH[_n] = ("psum", [128, 512], "float32")
for _u in range(2):
    SCRATCH["kf%d" % _u] = ("sbuf", [128, 4], "float32")
    SCRATCH["ot%d" % _u] = ("sbuf", [128, 96], "float32")
    SCRATCH["om%d" % _u] = ("sbuf", [128, 96], "float32")
    SCRATCH["off%d" % _u] = ("sbuf", [128, 96], "uint16")
    SCRATCH["pw%d" % _u] = ("sbuf", [128, 4 * RT], "float32")
    SCRATCH["pk%d" % _u] = ("sbuf", [128, 4 * TQ], "float32")
    SCRATCH["at%d" % _u] = ("sbuf", [128, 4 * TQ], "bfloat16")
    SCRATCH["ac%d" % _u] = ("sbuf", [128, TQ], "float8_e4m3fn_x4")
    SCRATCH["as%d" % _u] = ("sbuf", [128, TQ], "uint8")

SEMAPHORES = ["l_k0", "l_k1", "l_rt", "l_qx", "l_vv", "l_kp", "l_qp",
              "q_k0", "q_k1", "q_rt", "q_qx", "q_vv",
              "r_kpf", "r_kp", "r_kw", "r_k0", "r_k1", "r_k2", "r_k3", "r_ks", "r_x", "r_q",
              "r_vc", "r_vs", "r_v1", "r_v2", "r_v3", "r_v4", "r_a10", "r_a11", "r_a20", "r_a21", "r_a30", "r_a31",
              "sent", "m_y0", "m_y1", "c_y0", "c_y1", "st0", "st1"]
for _u in range(2):
    SEMAPHORES += ["%s%d" % (_n, _u) for _n in ("o_k", "o_t", "o_m", "o_o", "rb")]
    SEMAPHORES += ["%s%d%d" % (_n, _u, _h) for _n in ("rl", "qa") for _h in range(2)]
    SEMAPHORES += ["%s%d%d" % (_n, _u, _b) for _n in ("m_p", "m_s", "c_p") for _b in range(4)]
    SEMAPHORES += ["%s%d%d%d" % (_n, _u, _b, _h) for _n in ("ga", "ad") for _b in range(4) for _h in range(2)]


def bits(es):
    return sum(1 << e for e in es)


def team(rank_core, topo):
    mine = topo.cores_of(rank_core)
    near = [c for c in mine if c != rank_core and topo.die(c) == topo.die(rank_core)]
    far = [c for c in mine if topo.die(c) != topo.die(rank_core)]
    return near[:3], far


def rank_program(g, core, T, topo):
    v, sc, pe, sy = g.vector, g.scalar, g.tensor, g.sync
    cores = list(T.cores)
    teams = [team(c, topo) for c in cores]
    r = None
    for i, c in enumerate(cores):
        if core == c or core in teams[i][0] or core in teams[i][1]:
            r = i
    if r is None:
        return
    me = cores[r]
    near, far = teams[r]
    relays = [far[0], near[0], far[1], near[1]]
    posts = [far[0], near[0], near[2], near[1]]
    out = topo.engines(me, cores[(r + 1) % N])
    every = topo.engines(me, far[0])
    stay = [e for e in every if e not in out]
    few = len(stay) // 2
    sent = [0]

    def worker(s, d):
        i = (s + d) % N
        return teams[i][0][d - 1] if d < 4 else cores[i]

    users = [worker(r, d) for d in (1, 2, 3, 4)]

    def wait(queue, name, n=1):
        queue.wait_ge(T.sem[name], n)

    def inc(ins, name, n=1):
        ins.then_inc(T.sem[name], n)

    def move(dsts, outs, src, sem, es):
        ids = []
        for c in dsts:
            a = topo.addr(c)
            ids.append(DstId(rid=a[0], pnc=a[1]))
        sent[0] += len(es)
        return RemoteDMATransfer(dst_ids=ids, dma_engine_mask=bits(es), remote_sem=T.sem[sem], srcs=[src], dsts=list(outs))

    def send(*moves):
        g.remote_dma_fused(list(moves), local_sem=T.sem["sent"])

    def by(t):
        return t.bitcast(dt.uint8)

    def offsets(u, kp, kp_event, q_event):
        kf, ot, om, off = T["kf%d" % u], T["ot%d" % u], T["om%d" % u], T["off%d" % u]
        wait(v, *kp_event)
        inc(v.tensor_copy(kf[:], kp[:]), "o_k%d" % u)
        wait(v, *q_event)
        wait(v, "o_k%d" % u)
        for b in range(4):
            inc(v.tensor_scalar(ot[:, 24 * b:24 * b + 24], T.qr[:], kf[:, b:b + 1], -128.0, AluOpType.subtract, AluOpType.max), "o_t%d" % u)
        wait(v, "o_t%d" % u, 4)
        inc(v.tensor_scalar(om[:], ot[:], 127.0, 128.0, AluOpType.min, AluOpType.add), "o_m%d" % u)
        wait(v, "o_m%d" % u)
        inc(v.tensor_copy(off[:], om[:]), "o_o%d" % u)

    def products(u, kc, ks, banks, events, events_x):
        for h in range(2):
            for b in (2 * h, 2 * h + 1):
                for e in events[b]:
                    wait(pe, *e)
                if b >= banks:
                    wait(pe, "c_p%d%d" % (u, b - banks))
                elif u:
                    wait(pe, "c_p%d%d" % (u - 1, b))
                    wait(pe, "c_p%d%d" % (u - 1, b + 2))
                inc(pe.matmul_mx(T[BANKS[b % banks]][:, 0:RT], kc[:, 128 * b:128 * b + 128], ks[:, 128 * b:128 * b + 128],
                                 T.xc[:, TQ:XW], T.xs[:, TQ:XW], True, True), "m_p%d%d" % (u, b))
            for e in events_x:
                wait(pe, *e)
            for b in (2 * h, 2 * h + 1):
                if u:
                    wait(pe, "ad%d%d0" % (u - 1, b))
                    wait(pe, "ad%d%d1" % (u - 1, b))
                inc(pe.matmul_mx(T["sb%d" % b][:, 0:TQ], kc[:, 128 * b:128 * b + 128], ks[:, 128 * b:128 * b + 128],
                                 T.xc[:, 0:TQ], T.xs[:, 0:TQ], True, True), "m_s%d%d" % (u, b))

    def copy_p(queue, u, b, banks):
        bank, window = T[BANKS[b % banks]][:, 0:RT], T["pw%d" % u][:, RT * b:RT * b + RT]
        wait(queue, "m_p%d%d" % (u, b))
        if queue is v:
            ins = v.tensor_copy(window, bank)
        else:
            ins = sc.activation(window, bank, ActivationFunctionType.Copy)
        inc(ins, "c_p%d%d" % (u, b))

    def pick(u, b, h):
        off, at = T["off%d" % u], 24 * b + 12 * h
        wait(sc, "c_p%d%d" % (u, b))
        inc(sc.activation(T["pk%d" % u][:, TQ * b + HALF * h:TQ * b + HALF * h + HALF],
                          T["pw%d" % u][:, RT * b:RT * b + RT].indirect(off[:, at:at + 12]), ActivationFunctionType.Copy), "ga%d%d%d" % (u, b, h))

    def picks(u, banks):
        copy_p(sc, u, 0, banks)
        wait(sc, "o_o%d" % u)
        for b, h in ((0, 0), (1, 0), (0, 1), (1, 1)):
            pick(u, b, h)
        copy_p(sc, u, 3, banks)
        for b, h in ((2, 0), (3, 0), (2, 1), (3, 1)):
            pick(u, b, h)

    def add(u, b, h):
        wait(v, "m_s%d%d" % (u, b))
        wait(v, "ga%d%d%d" % (u, b, h))
        inc(v.tensor_tensor(T["at%d" % u][:, 4 * HALF * h + b:4 * HALF * (h + 1):4], T["sb%d" % b][:, HALF * h:HALF * h + HALF],
                            T["pk%d" % u][:, TQ * b + HALF * h:TQ * b + HALF * h + HALF], AluOpType.add), "ad%d%d%d" % (u, b, h))

    def relu(u, b, hs, sem):
        col = T["at%d" % u][:, 4 * HALF * hs[0] + b:4 * HALF * (hs[-1] + 1):4]
        for h in hs:
            wait(v, "ad%d%d%d" % (u, b, h))
        inc(v.tensor_scalar(col, col, 0.0, 0.03125, AluOpType.max, AluOpType.mult), sem)

    def elementwise(u, banks):
        copy_p(v, u, 1, banks)
        add(u, 0, 0)
        add(u, 1, 0)
        copy_p(v, u, 2, banks)
        add(u, 0, 1)
        add(u, 1, 1)
        relu(u, 0, (0, 1), "rb%d" % u)
        relu(u, 1, (0, 1), "rb%d" % u)
        for h in range(2):
            for b in (2, 3):
                add(u, b, h)
                relu(u, b, (h,), "rl%d%d" % (u, h))
            if h == 0:
                wait(v, "rb%d" % u, 2)
            wait(v, "rl%d%d" % (u, h), 2)
            a, e = HALF * h, HALF * h + HALF
            inc(v.quantize_mx(T["ac%d" % u][:, a:e], T["as%d" % u][:, a:e], T["at%d" % u][:, 4 * a:4 * e]), "qa%d%d" % (u, h))

    if core in posts:
        c = users[posts.index(core)]
        wait(g, "r_kpf", len(every))
        send(move([c], [T.kpr[:]], T.kpf[:], "r_kp", out))
    if core in relays:
        b = relays.index(core)
        wait(g, "r_kw", len(stay) if b < 2 else few)
        send(move(users, [by(T.kc[:, 128 * b:128 * b + 128])] * 4, by(T.kw[:]), "r_k%d" % b, out))
    per = len(out) // 4
    for c, name, own, there, f in ((far[2], "r_vc", T.vo, T.vr, by), (far[3], "r_vs", T.vos, T.vrs, lambda t: t)):
        if core == c:
            wait(g, name, len(stay))
            send(*[move([cores[(r + d) % N]], [f(there[:, 128 * (d - 1):128 * d])], f(own[:]), "r_v%d" % d, out[per * (d - 1):per * d])
                   for d in (1, 2, 3, 4)])
    if core in far:
        wait(g, "sent", sent[0])
        return

    keys = [[("r_ks", len(out)), ("r_k%d" % b, len(out))] for b in range(4)]

    if core in near:
        d = near.index(core) + 1
        offsets(0, T.kpr, ("r_kp", len(out)), ("r_q", len(stay)))
        products(0, T.kc, T.kcs, 4, [keys[0] + [("r_x", 2 * len(every))]] + keys[1:], [])
        picks(0, 4)
        elementwise(0, 4)
        a = TQ * (d - 1)
        for h in range(2):
            wait(g, "qa0%d" % h)
            i, e = HALF * h, HALF * h + HALF
            send(move([me], [by(T.ar[:, a + i:a + e])], by(T.ac0[:, i:e]), "r_a%d%d" % (d, h), every))
            send(move([me], [T.ars[:, a + i:a + e]], T.as0[:, i:e], "r_a%d%d" % (d, h), every))
        wait(g, "sent", sent[0])
        return

    inc(sy.dma_start(T.kpo[:], T.kp[:]), "l_kp", 16)
    inc(sy.dma_start(T.kyb[:, 0:1024], T.ky[:, 0:1024]), "l_k0", 16)
    inc(sy.dma_start(T.kyb[:, 1024:2048], T.ky[:, 1024:2048]), "l_k1", 16)
    inc(sy.dma_start(T.rtb[:], T.rt[:]), "l_rt", 16)
    for q in range(8):
        inc(sc.dma_start(T.qr[16 * q:16 * q + 16, :], T.qp[:]), "l_qp", 16)
    inc(sc.dma_start(T.qxb[:], T.qx[:]), "l_qx", 16)
    inc(sc.dma_start(T.vvb[:], T.vv[:]), "l_vv", 16)

    wait(g, "l_kp", 16)
    send(move(posts, [T.kpf[:]] * 4, T.kpo[:], "r_kpf", every))

    def piece(b, es):
        return move([relays[b]], [by(T.kw[:])], by(T.ko[:, 128 * b:128 * b + 128]), "r_kw", es)

    wait(g, "q_k0")
    send(piece(0, out), piece(1, stay))
    wait(g, "q_k1")
    send(piece(2, stay[:few]), piece(3, stay[few:]), move(users, [T.kcs[:]] * 4, T.kos[:], "r_ks", out))
    wait(g, "l_qp", 128)
    send(move(near, [T.qr[:]] * 3, T.qr[:], "r_q", stay))
    wait(g, "q_rt")
    wait(g, "q_qx")
    for a in (by(T.xc[:]), T.xs[:]):
        send(move(near[::-1], [a] * 3, a, "r_x", every))
    wait(g, "q_vv")
    send(move([far[2]], [by(T.vo[:])], by(T.vo[:]), "r_vc", stay))
    send(move([far[3]], [T.vos[:]], T.vos[:], "r_vs", out))
    wait(g, "sent", sent[0])

    for name, codes, plane, tile in (("k0", T.ko[:, 0:256], T.kos[:, 0:256], T.kyb[:, 0:1024]),
                                     ("k1", T.ko[:, 256:512], T.kos[:, 256:512], T.kyb[:, 1024:2048]),
                                     ("rt", T.xc[:, TQ:XW], T.xs[:, TQ:XW], T.rtb[:]),
                                     ("qx", T.xc[:, 0:TQ], T.xs[:, 0:TQ], T.qxb[:])):
        wait(v, "l_" + name, 16)
        inc(v.quantize_mx(codes, plane, tile), "q_" + name)
    offsets(0, T.kpo, ("l_kp", 16), ("l_qp", 128))
    wait(v, "l_vv", 16)
    inc(v.quantize_mx(T.vo[:], T.vos[:], T.vvb[:]), "q_vv")
    elementwise(0, 4)
    offsets(1, T.kpr, ("r_kp", len(out)), ("l_qp", 128))
    elementwise(1, 2)

    picks(0, 4)
    picks(1, 2)

    def value(vc, vs, ac, as_, a, h, start, stop):
        i, e = a + HALF * h, a + HALF * h + HALF
        ins = pe.matmul_mx(T["yb%d" % h][:, 0:HALF], vc, vs, ac[:, i:e], as_[:, i:e], start, stop)
        if stop:
            inc(ins, "m_y%d" % h)

    def slot(d):
        return T.vr[:, 128 * (d - 1):128 * d], T.vrs[:, 128 * (d - 1):128 * d]

    products(0, T.ko, T.kos, 4, [[("q_k0", 1), ("q_rt", 1)], [], [("q_k1", 1)], []], [("q_qx", 1)])
    for e in ("qa00", "qa01", "q_vv", "c_p02", "c_p03"):
        wait(pe, e)
    for h in range(2):
        value(T.vo[:], T.vos[:], T.ac0, T.as0, 0, h, True, False)
    products(1, T.kc, T.kcs, 2, keys, [])
    for h in range(2):
        for d in (4, 3, 1, 2):
            wait(pe, "r_v%d" % d, 2 * per)
            if d == 4:
                wait(pe, "qa1%d" % h)
                value(*slot(d), T.ac1, T.as1, 0, h, False, False)
            else:
                wait(pe, "r_a%d%d" % (d, h), 2 * len(every))
                value(*slot(d), T.ar, T.ars, TQ * (d - 1), h, False, d == 2)

    wait(sc, "m_y0")
    inc(sc.activation(T.ysb[:, 0:HALF], T.yb0[:, 0:HALF], ActivationFunctionType.Copy), "c_y0")
    wait(sc, "c_y0")
    inc(sc.dma_start(T.y[:, 0:HALF], T.ysb[:, 0:HALF]), "st0", 16)
    wait(v, "m_y1")
    inc(v.tensor_copy(T.ysb[:, HALF:TQ], T.yb1[:, 0:HALF]), "c_y1")
    wait(sy, "c_y1")
    inc(sy.dma_start(T.y[:, HALF:TQ], T.ysb[:, HALF:TQ]), "st1", 16)
    wait(sc, "st0", 16)
    wait(sy, "st1", 16)
